import numpy as np, ml_dtypes
CORES = [7,39,87,119,135,167,215,247,263,295,343,375,391,423,471,503]
N = 16
J, Q = 512, 2048
def entries(a): return a.T.reshape(-1)
def pack(v, P): return np.ascontiguousarray(np.asarray(v, np.int32).reshape(-1, P).T)
def split(rng, total, parts):
    c = np.sort(rng.integers(0, total + 1, parts - 1)); return np.diff(np.concatenate([[0], c, [total]]))
def lists(rng, how):
    s = np.concatenate([[0], rng.integers(1 - Q // 2, Q // 2 + 1, N - 1), [int(rng.integers(1 - Q // 2, 1))]])
    if how == "early": s[1:] = -Q; s[N] = -2 * Q
    if how == "late": s[1:] = Q; s[N] = 0
    if how == "long":
        z = int(rng.integers(1, N - 1)); s[1:z] = -rng.integers(1, Q, z - 1); s[z] = -Q; s[z + 1] = Q; s[z + 2:N] = rng.integers(1, Q, N - z - 2); s[N] = -int(rng.integers(0, Q - s[N - 1] + 1))
    if how == "sway":
        z = int(rng.integers(1, N - 2)); e = int(rng.integers(z + 1, N - 1)); s[1:] = -rng.integers(Q // 2 + 1, Q, N); s[z + 1:e + 1] = rng.integers(Q // 2 + 1, Q - 1, e - z); s[e + 1] = s[e] - Q; s[N] = s[N - 1] - Q + int(rng.integers(1, -s[N - 1]))
    tot = Q + np.diff(s)
    L = np.stack([split(rng, int(t), J) for t in tot])
    if how == "gaps":
        L = np.zeros((N, J), np.int64)
        for r in range(N): m = 1 if r & 1 else 8; L[r, 1 + rng.permutation(J - 2)[:m]] = split(rng, int(tot[r]), m)
    if how == "long":
        L = np.zeros((N, J), np.int64); L[np.arange(N), rng.integers(0, J, N)] = tot
    return {"ln": np.stack([pack(l, 16) for l in L])}
def setup_inputs(rng):
    return dict({"x": rng.standard_normal((N, 128, J), dtype=np.float32).astype(ml_dtypes.bfloat16)}, **lists(rng, "uniform"))
def setup_inputs_early(rng):
    d = setup_inputs(rng); d.update(lists(rng, "early"))
    for k in ("x",): d[k] = (d[k].astype(np.float32) * 1048576.0).astype(d[k].dtype)
    return d
def setup_inputs_gaps(rng):
    d = setup_inputs(rng); d.update(lists(rng, "gaps"))
    for k in ("x",): d[k] = (d[k].astype(np.float32) * (1 / 1024.0)).astype(d[k].dtype)
    return d
def setup_inputs_late(rng):
    d = setup_inputs(rng); d.update(lists(rng, "late"))
    return d
def setup_inputs_long(rng):
    d = setup_inputs(rng); d.update(lists(rng, "long"))
    return d
def setup_inputs_sway(rng):
    d = setup_inputs(rng); d.update(lists(rng, "sway"))
    return d
def check_inputs(x):
    bad = []
    if x["ln"].min() < 0 or x["ln"].max() >= N * Q + 1: bad.append("ln out of range")
    if int(x["ln"].sum()) > N * Q: bad.append("the lengths come to more than N * Q")
    c = np.concatenate([[0], np.cumsum([int(a.sum()) for a in x["ln"]])])
    if any(c[r] < (r - 1) * Q or c[r + 1] > (r + 2) * Q for r in range(N)): bad.append("the sums of the lengths before or up to a rank leave their bounds")
    return bad
def reference(x, ln):
    got = np.concatenate([np.repeat(x[r], entries(ln[r]), axis=1) for r in range(N)], axis=1)[:, :N * Q]
    Y = np.zeros((128, N * Q), x.dtype); Y[:, :got.shape[1]] = got
    return {"y": np.stack([Y[:, Q * r:Q * r + Q] for r in range(N)])}

import numpy as np
from concourse.bass import DstId, RemoteDMATransfer
from concourse.mybir import dt, AluOpType, AxisListType, ActivationFunctionType

J, Q, R, H = 512, 2048, 16, 8
MAGIC = 12582912.0

SCRATCH = {
    "lists": ("dram", [H + 1, 128, 4], "int32"),
    "tot": ("dram", [128, 4], "int32"),
    "win": ("sbuf", [128, 3 * J + 8], "bfloat16"),
    "yb": ("sbuf", [128, Q], "bfloat16"),
    "lw": ("sbuf", [128, 96], "int32"),
    "lf": ("sbuf", [128, 104], "float32"),
    "bi": ("sbuf", [128, 4 * H + 4], "int32"),
    "bf": ("sbuf", [128, 4 * H + 4], "float32"),
    "rs": ("sbuf", [128, 4], "float32"),
    "ic": ("sbuf", [128, 128], "bfloat16"),
    "sg": ("sbuf", [128, 128], "bfloat16"),
    "pi": ("sbuf", [128, 4], "int32"),
    "gq": ("sbuf", [128, 4], "int32"),
    "gm": ("sbuf", [128, 4], "int32"),
    "go": ("sbuf", [128, 4], "int32"),
    "goff": ("sbuf", [128, 8], "uint16"),
    "pf": ("sbuf", [128, 4], "float32"),
    "p7": ("sbuf", [128, 4], "float32"),
    "od": ("sbuf", [128, 128], "float32"),
    "ob": ("sbuf", [128, 128], "bfloat16"),
    "os": ("sbuf", [128, 96], "float32"),
    "t1": ("sbuf", [128, 128], "bfloat16"),
    "t2": ("sbuf", [128, 128], "bfloat16"),
    "ih": ("sbuf", [128, 128], "float16"),
    "uh": ("sbuf", [128, 128], "float16"),
    "le": ("sbuf", [128, 128], "float32"),
    "gt": ("sbuf", [128, 128], "float32"),
    "wf": ("sbuf", [128, 112], "float32"),
    "wk": ("sbuf", [128, 16], "float32"),
    "ee": ("sbuf", [128, 12], "float32"),
    "aa": ("sbuf", [128, 12], "float32"),
    "nb": ("sbuf", [128, 12], "float32"),
    "oh": ("sbuf", [128, 12 * 128], "bfloat16"),
    "th": ("sbuf", [128, 12 * 64], "bfloat16"),
    "yh": ("sbuf", [128, 128], "float16"),
    "hr": ("sbuf", [128, 128], "float16"),
    "ofa": ("sbuf", [128, 64], "uint16"),
    "ofb": ("sbuf", [128, 64], "uint16"),
    "pw": ("psum", [128, 512], "float32"),
    "pd": ("psum", [128, 512], "float32"),
    "py": ("psum", [128, 512], "float32"),
    "poa": ("psum", [128, 512], "float32"),
    "pob": ("psum", [128, 512], "float32"),
}
SCRATCH["ones1"] = SCRATCH.pop("os")

SEMAPHORES = (["ldln", "ldx", "ldow", "ldnb0", "ldnb1", "ldin", "ldt", "gi", "vc", "arr", "xin", "t01", "snt", "lf1", "pew",
               "wf1", "wk1", "bf1", "bf2", "rs1", "ped", "ee1", "aa1", "nb1", "pey", "yh1", "peb", "pea", "fb1", "fa1",
               "gv0", "gv1", "gs0", "gs1", "st", "st2"]
              + ["oh%d" % m for m in range(12)] + ["th%d" % m for m in range(12)])


def engines(mask, n):
    bits = [1 << i for i in range(16) if (mask >> i) & 1]
    out = 0
    for b in bits[:n]:
        out |= b
    return out


def plan(T, topo):
    cores = T.cores
    rk = [topo.rack(topo.host(c)) for c in cores]
    dests = []
    for r in range(R):
        ds = []
        for d in range(R):
            if d == r:
                continue
            near = abs(d - r) == 1
            same = rk[d] == rk[r]
            if near or (same and (rk[r] == rk[0] or d > r)):
                ds.append(d)
        dests.append(ds)
    relay = {}
    for d in range(R):
        if rk[d] == rk[0]:
            continue
        for s in range(R):
            if rk[s] == rk[0] and topo.may_write(cores[s], cores[d]) and topo.chip(cores[s]) == topo.chip(cores[d]):
                relay[s] = d
    return rk, dests, relay


def rank_program(g, core, T, topo):
    rank = T.rank_of(core)
    if rank is None:
        return
    r = rank
    A = AluOpType
    F = ActivationFunctionType
    V, S, P, Y = g.vector, g.scalar, g.tensor, g.sync
    sem = T.sem
    cores = T.cores
    rk, dests, relay = plan(T, topo)
    first_rack = rk[r] == rk[0]
    r0 = rk.index(rk[r])

    def slot(src, dst):
        return src - rk.index(rk[src]) if rk[src] == rk[dst] else H

    def dst_id(d):
        rid, pid = topo.addr(cores[d], core)
        return DstId(rid=rid, pnc=pid)

    def common(ds):
        m = 0xFFFF
        for d in ds:
            m &= topo.mask(core, cores[d])
        return m

    blocks = [t for t in (r - 1, r, r + 1) if 0 <= t < R]
    nbrs = [t for t in blocks if t != r]
    nb = len(blocks)
    n = 32 * nb
    step = n // 8
    first = blocks[0]
    w0 = J * (first - (r - 1))
    w1 = J * (blocks[-1] - (r - 1) + 1)
    in_rack = [t for t in range(first) if rk[t] == rk[r]]
    has_tot = not first_rack
    has_base = has_tot or len(in_rack) > 0

    NE_L, NE_F, NE_X = 2, 8, 8
    n_arr = NE_L * len([s for s in range(R) if r in dests[s]])
    n_xin = NE_X * len(nbrs)

    Y.dma_start(T.lists[r - r0], T.ln[:]).then_inc(sem.ldln, 16)
    oc = 32 * (r - first)
    Y.dma_start(T.lw[0:16, oc:oc + 32], T.ln[:]).then_inc(sem.ldow, 16)
    S.dma_start(T.win[:, J:2 * J], T.x[:]).then_inc(sem.ldx, 16)

    g.iota(T.sg[:], [[0, 8], [1, 16]], -7, 0, allow_small_or_imprecise_dtypes=True).then_inc(sem.gi, 1)
    g.iota(T.ic[:], [[1, 128]], 0, 0, allow_small_or_imprecise_dtypes=True).then_inc(sem.gi, 1)
    g.iota(T.pi[:, 0:1], [[0, 1]], 0, 1).then_inc(sem.gi, 1)

    n_snt = [0]
    mine = T.lists[r - r0]
    g.wait_ge(sem.ldln, 16)
    ds = dests[r]
    g.remote_dma_fused([RemoteDMATransfer(
        dst_ids=[dst_id(d) for d in ds], dma_engine_mask=engines(common(ds), NE_L), remote_sem=sem.arr,
        srcs=[mine], dsts=[T.lists[slot(r, d)] for d in ds], alu_op=0)], local_sem=sem.snt)
    n_snt[0] += NE_L

    def send_x(to):
        g.remote_dma_fused([RemoteDMATransfer(
            dst_ids=[dst_id(d) for d in to], dma_engine_mask=engines(common(to), NE_X), remote_sem=sem.xin,
            srcs=[T.win[:, J:2 * J]],
            dsts=[T.win[:, J * (r - d + 1):J * (r - d + 2)] for d in to], alu_op=0)], local_sem=sem.snt)
        n_snt[0] += NE_X

    g.wait_ge(sem.ldx, 16)
    if r in relay:
        later = [t for t in nbrs if t < r]
        send_x([t for t in nbrs if t > r])
        d = relay[r]
        g.wait_ge(sem.arr, n_arr)
        upto = [t for t in range(R) if rk[t] == rk[r] and t < d - 1]
        g.remote_dma_fused([RemoteDMATransfer(
            dst_ids=[dst_id(d)], dma_engine_mask=engines(common([d]), NE_F), remote_sem=sem.t01,
            srcs=[T.lists[t - r0] for t in upto], dsts=[T.tot[:]], alu_op=1)], local_sem=sem.snt)
        n_snt[0] += NE_F
        if later:
            send_x(later)
    else:
        send_x(nbrs)

    c = [0]

    def k(ins):
        ins.then_inc(sem.vc, 1)
        c[0] += 1

    k(V.memset(T.od[:], 0.0625))
    k(V.memset(T.ob[:], 1.0))
    k(V.memset(T.ones1[:], 1.0))
    k(V.memset(T.lf[0:16, 0:1], 0.0))
    k(V.memset(T.wf[:, n:n + 16], 0.0))
    k(V.memset(T.win[:, w1:w1 + 8], 0.0))
    V.wait_ge(sem.gi, 3)
    k(V.tensor_copy(T.pf[:, 0:1], T.pi[:, 0:1]))
    k(V.tensor_scalar(T.p7[:, 0:1], T.pi[:, 0:1], -7.0, None, A.add))
    k(V.tensor_scalar(T.gq[:, 0:1], T.pi[:, 0:1], 4, None, A.arith_shift_right))
    V.wait_ge(sem.vc, c[0])
    k(V.tensor_scalar(T.le[0:16, :], T.sg[0:16, :], T.p7[0:16, 0:1], 0.0625, A.is_ge, A.mult))
    k(V.tensor_scalar(T.gt[0:16, :], T.sg[0:16, :], T.p7[0:16, 0:1], 0.0625, A.is_lt, A.mult))
    k(V.tensor_scalar(T.gm[:, 0:1], T.gq[:, 0:1], 16 - step, None, A.mult))
    k(V.tensor_scalar(T.t1[:], T.ic[:], T.pf[:, 0:1], 0.5, A.is_gt, A.mult))
    k(V.tensor_scalar(T.t2[:], T.ic[:], T.pf[:, 0:1], 0.5, A.is_ge, A.mult))
    V.wait_ge(sem.vc, c[0])
    k(V.tensor_tensor(T.go[:, 0:1], T.pi[:, 0:1], T.gm[:, 0:1], A.subtract))
    k(V.tensor_tensor(T.ih[:], T.t2[:], T.t1[:], A.subtract))
    k(V.tensor_tensor(T.uh[:], T.t2[:], T.t1[:], A.add))
    V.wait_ge(sem.vc, c[0])
    k(V.tensor_copy(T.goff[:, 0:1], T.go[:, 0:1]))
    V.wait_ge(sem.vc, c[0])
    n_vc = c[0]

    Y.wait_ge(sem.arr, n_arr)
    S.wait_ge(sem.arr, n_arr)
    for i, t in enumerate(nbrs):
        q = (Y, S)[i]
        o = 32 * (t - first)
        q.dma_start(T.lw[0:16, o:o + 32], T.lists[slot(t, r)]).then_inc(sem["ldnb%d" % i], 16)
    if in_rack:
        m = len(in_rack)
        Y.dma_start(T.bi[:, 4:4 + 4 * m], T.lists[0:m]).then_inc(sem.ldin, 16)
    if has_tot:
        Y.wait_ge(sem.t01, NE_F)
        Y.dma_start(T.bi[:, 0:4], T.tot[:]).then_inc(sem.ldt, 16)

    V.wait_ge(sem.ldow, 16)
    for i in range(len(nbrs)):
        V.wait_ge(sem["ldnb%d" % i], 16)
    V.tensor_copy(T.lf[0:16, 1:1 + n], T.lw[0:16, 0:n]).then_inc(sem.lf1, 1)
    b0, b1 = (0 if has_tot else 4), 4 + 4 * len(in_rack)
    if in_rack:
        V.wait_ge(sem.ldin, 16)
        V.tensor_copy(T.bf[:, 4:b1], T.bi[:, 4:b1]).then_inc(sem.bf1, 1)
    V.wait_ge(sem.pew, 1)
    V.tensor_tensor_scan(T.wf[:, 0:n], T.ones1[:, 0:n], T.pw[:, 0:n], -128.0 * r - 15.0 / 32.0,
                         A.mult, A.add).then_inc(sem.wf1, 1)
    V.wait_ge(sem.wf1, 1)
    V.tensor_copy(T.wk[:], T.wf[:, 0:n + 16].indirect(T.goff[:, 0:1])).then_inc(sem.wk1, 1)
    if has_base:
        if in_rack:
            V.wait_ge(sem.bf1, 1)
        if has_tot:
            V.wait_ge(sem.ldt, 16)
            V.tensor_copy(T.bf[:, 0:4], T.bi[:, 0:4]).then_inc(sem.bf2, 1)
            V.wait_ge(sem.bf2, 1)
        V.tensor_reduce(T.rs[:, 0:1], T.bf[:, b0:b1], AxisListType.X, A.add).then_inc(sem.rs1, 1)
    V.wait_ge(sem.wk1, 1)
    if has_base:
        V.wait_ge(sem.ped, 1)
        V.tensor_scalar(T.ee[:, 0:step], T.wk[:, 0:step], T.pd[:, 0:1], -15.0 / 32.0, A.add, A.max).then_inc(sem.ee1, 1)
    else:
        V.tensor_scalar(T.ee[:, 0:step], T.wk[:, 0:step], -15.0 / 32.0, None, A.max).then_inc(sem.ee1, 1)
    V.wait_ge(sem.ee1, 1)
    V.tensor_scalar(T.aa[:, 0:step], T.ee[:, 0:step], MAGIC, -MAGIC, A.add, A.add).then_inc(sem.aa1, 1)
    V.wait_ge(sem.aa1, 1)
    V.tensor_tensor(T.nb[:, 0:step], T.aa[:, 0:step], T.ee[:, 0:step], A.subtract).then_inc(sem.nb1, 1)
    for m in range(step):
        V.tensor_scalar(T.oh[:, 128 * m:128 * m + 128], T.ic[:], T.aa[:, m:m + 1], None,
                        A.is_equal).then_inc(sem["oh%d" % m], 1)
    S.wait_ge(sem.gi, 3)
    S.wait_ge(sem.nb1, 1)
    for m in range(step):
        S.activation(T.th[:, 64 * m:64 * m + 64], T.sg[:, 0:64], F.Sign, bias=T.nb[:, m:m + 1],
                     scale=0.0625).then_inc(sem["th%d" % m], 1)

    P.wait_ge(sem.vc, n_vc)
    P.wait_ge(sem.lf1, 1)
    P.matmul(T.pw[:, 0:n], T.le[0:16, :], T.lf[0:16, 1:1 + n], True, False)
    P.matmul(T.pw[:, 0:n], T.gt[0:16, :], T.lf[0:16, 0:n], False, True).then_inc(sem.pew, 1)
    if has_base:
        P.wait_ge(sem.rs1, 1)
        P.matmul(T.pd[:, 0:1], T.od[:], T.rs[:, 0:1], True, True).then_inc(sem.ped, 1)
    for m in range(step):
        P.wait_ge(sem["oh%d" % m], 1)
        P.wait_ge(sem["th%d" % m], 1)
        ins = P.matmul(T.py[:, 0:64], T.oh[:, 128 * m:128 * m + 128], T.th[:, 64 * m:64 * m + 64], m == 0, m == step - 1)
        if m == step - 1:
            ins.then_inc(sem.pey, 1)
    P.wait_ge(sem.yh1, 3)
    P.matmul(T.pob[:, 0:64], T.yh[:], T.ih[:, 64:128], True, False)
    P.matmul(T.pob[:, 0:64], T.hr[:], T.uh[:, 64:128], False, True).then_inc(sem.peb, 1)
    P.matmul(T.poa[:, 0:64], T.yh[:], T.ih[:, 0:64], True, False)
    P.matmul(T.poa[:, 0:64], T.hr[:], T.uh[:, 0:64], False, True).then_inc(sem.pea, 1)

    V.wait_ge(sem.pey, 1)
    V.tensor_copy(T.yh[:, 0:64], T.py[:, 0:64]).then_inc(sem.yh1, 1)
    V.tensor_copy(T.yh[:, 64:128], T.py[:, 0:64]).then_inc(sem.yh1, 1)
    V.tensor_scalar(T.hr[:], T.ob[:], T.py[:, 15:16], None, A.mult).then_inc(sem.yh1, 1)
    V.wait_ge(sem.peb, 1)
    V.tensor_copy(T.ofb[:], T.pob[:, 0:64]).then_inc(sem.fb1, 1)
    V.wait_ge(sem.pea, 1)
    V.tensor_copy(T.ofa[:], T.poa[:, 0:64]).then_inc(sem.fa1, 1)

    win = T.win[:, w0:w1 + 8]
    V.wait_ge(sem.ldx, 16)
    V.wait_ge(sem.xin, n_xin)
    V.wait_ge(sem.fa1, 1)
    for i in range(2):
        V.tensor_copy(T.yb[:, 512 * i:512 * i + 512],
                      win.indirect(T.ofa[:, 32 * i:32 * i + 32])).then_inc(sem["gv%d" % i], 1)
    S.wait_ge(sem.vc, n_vc)
    S.wait_ge(sem.ldx, 16)
    S.wait_ge(sem.xin, n_xin)
    S.wait_ge(sem.fb1, 1)
    for i in range(2):
        o = 1024 + 512 * i
        S.activation(T.yb[:, o:o + 512], win.indirect(T.ofb[:, 32 * i:32 * i + 32]), F.Copy,
                     bias=-0.0).then_inc(sem["gs%d" % i], 1)
    for i in range(2):
        Y.wait_ge(sem["gv%d" % i], 1)
        Y.dma_start(T.y[:, 512 * i:512 * i + 512], T.yb[:, 512 * i:512 * i + 512]).then_inc(sem.st, 16)
        o = 1024 + 512 * i
        q = (Y, S)[i]
        q.wait_ge(sem["gs%d" % i], 1)
        q.dma_start(T.y[:, o:o + 512], T.yb[:, o:o + 512]).then_inc((sem.st, sem.st2)[i], 16)
    Y.wait_ge(sem.st, 48)
    S.wait_ge(sem.st2, 16)
    g.wait_ge(sem.snt, n_snt[0])
